import numpy as np
import ml_dtypes


def mxq(x, axis, fmt="e4m3"):
    dtype, down = {"e4m3": (ml_dtypes.float8_e4m3fn, 7), "e5m2": (ml_dtypes.float8_e5m2, 14)}[fmt]
    v = np.moveaxis(np.asarray(x, np.float32).astype(ml_dtypes.bfloat16).astype(np.float64), axis, -1)
    blocks = v.reshape(v.shape[:-1] + (-1, 32))
    amax = np.abs(blocks).max(-1, keepdims=True)
    byte = np.maximum(np.where(amax > 0, np.frexp(amax)[1] - 1 + 127, 0) - down, 1)
    scale = np.exp2(byte - 127.0)
    codes = (blocks / scale).astype(np.float32).astype(dtype).astype(np.float64)
    return np.moveaxis((codes * scale).reshape(v.shape), -1, axis)


WIDE = False


def mx_kscale(k):
    if not WIDE:
        return np.ones(k)
    levels = np.array([10, -10, 5, -5, 0])
    if k % 512:
        return np.exp2(np.random.permutation(np.resize(levels, k // 32))).repeat(32)
    a = np.empty((k // 512, 16))
    for p in range(k // 512):
        a[p, :8] = np.random.permutation(np.resize(levels, 8))
        for g in range(8):
            far = levels[np.abs(levels - a[p, g]) >= 10]
            a[p, g + 8] = far[np.random.randint(len(far))]
    return np.exp2(a.ravel()).repeat(32)


def f64(x):
    return np.asarray(x).astype(np.float64)


def striped8(idx):
    return np.asarray(idx).reshape(8, -1, 16).transpose(0, 2, 1).reshape(128, -1).astype(np.uint16)


def unstriped8(offs):
    return offs.reshape(8, 16, -1).transpose(0, 2, 1).reshape(8, -1).astype(np.int64)


def pick8(x, idx, run):
    r = np.arange(len(x))
    return x[r[:, None], idx[r % (8 * run) // run]]


E2M1 = np.array([0.0, 0.5, 1.0, 1.5, 2.0, 3.0, 4.0, 6.0, -0.0, -0.5, -1.0, -1.5, -2.0, -3.0, -4.0, -6.0])


def pack_weight(w, fmt):
    k, n = w.shape
    w = f64(np.asarray(w, np.float32).astype(ml_dtypes.bfloat16)).reshape(k // 32, 32, n)
    amax = np.abs(w).max(1)
    if fmt == "e4m3":
        byte = np.frexp(amax)[1] - 1 + 127 - 7
    else:
        mant, ex = np.frexp(amax / 6.0)
        byte = np.where(mant > 0.5, ex, ex - 1) + 127
    byte = np.clip(np.where(amax > 0, byte, 1), 1, 254)
    scaled = (w * np.exp2(127.0 - byte)[:, None, :]).reshape(k, n).astype(np.float32)
    by_word = np.ascontiguousarray(scaled.reshape(k // 512, 128, 4, n).transpose(0, 1, 3, 2))
    if fmt == "e4m3":
        words = by_word.astype(ml_dtypes.float8_e4m3fn).view(np.uint8)
    else:
        c = by_word.astype(ml_dtypes.float4_e2m1fn).view(np.uint8) & 0xF
        words = (c[..., 0::2] | (c[..., 1::2] << 4)).reshape(k // 512, 128, 2 * n)
    return np.ascontiguousarray(words), np.ascontiguousarray(byte.astype(np.uint8).reshape(k // 512, 16, n))


def unpack_weight(words, scales, fmt):
    g, _, n = scales.shape
    words = np.ascontiguousarray(words).reshape(g, 128, n, -1)
    if fmt == "e4m3":
        vals = words.view(ml_dtypes.float8_e4m3fn).astype(np.float64)
    else:
        nib = np.empty((g, 128, n, 4), np.uint8)
        nib[..., 0::2] = words & 0xF
        nib[..., 1::2] = words >> 4
        vals = E2M1[nib]
    vals = vals * np.repeat(np.exp2(scales.astype(np.float64) - 127.0), 8, axis=1)[..., None]
    return vals.transpose(0, 1, 3, 2).reshape(g * 512, n)


D, K, T, U, X, I, O, Q = 512, 512, 1024, 1024, 1024, 512, 2048, 128


def setup_inputs():
    n = np.random.standard_normal
    idx = np.stack([np.random.permutation(X)[:I] for _ in range(8)])
    idx2 = np.stack([np.random.permutation(O)[:I] for _ in range(8)])
    idx3 = np.stack([np.random.permutation(O)[:I] for _ in range(8)])
    idx4 = np.stack([np.random.permutation(X)[:I] for _ in range(8)])
    fd = mx_kscale(D)
    fk = mx_kscale(K)
    wqp = pack_weight(n((D, K)) * 1.0 / np.sqrt(D) * fd[:, None] * fk, "e4m3")
    cachep = pack_weight(n((K, T)) * 1.0 / np.sqrt(K) / fk[:, None], "e4m3")
    draftp = pack_weight(n((K, U)) * 1.0 / np.sqrt(K) / fk[:, None], "e2m1")
    archp = pack_weight(n((D, X)) * 1.0 / np.sqrt(D) * fd[:, None], "e4m3")
    return {
        "states": (n((D, Q)) * 0.95 / fd[:, None]).astype(np.float32),
        "wq_words": wqp[0],
        "wq_scales": wqp[1],
        "cache_words": cachep[0],
        "cache_scales": cachep[1],
        "draft_words": draftp[0],
        "draft_scales": draftp[1],
        "arch_words": archp[0],
        "arch_scales": archp[1],
        "offs": striped8(idx),
        "offs2": striped8(idx2),
        "offs3": striped8(idx3),
        "offs4": striped8(idx4),
    }


def reference(states, wq_words, wq_scales, cache_words, cache_scales, draft_words, draft_scales, arch_words, arch_scales, offs, offs2, offs3, offs4):
    idx = unstriped8(offs)
    idx2 = unstriped8(offs2)
    idx3 = unstriped8(offs3)
    idx4 = unstriped8(offs4)
    wqu = unpack_weight(wq_words, wq_scales, "e4m3")
    cacheu = unpack_weight(cache_words, cache_scales, "e4m3")
    draftu = unpack_weight(draft_words, draft_scales, "e2m1")
    archu = unpack_weight(arch_words, arch_scales, "e4m3")
    statesq = mxq(f64(states), 0, "e4m3")
    qv = wqu.T @ statesq
    qvq = mxq(qv, 0, "e4m3")
    a = qvq.T @ cacheu
    b = qvq.T @ draftu
    c0 = statesq.T @ archu
    ab = np.concatenate([a, b], axis=1)
    f1 = np.zeros((Q, O))
    f1[np.arange(Q)[:, None], idx2[np.arange(Q) % 128 // 16]] = pick8(c0, idx, 16)
    mo = np.maximum(ab, f1)
    f2 = np.zeros((Q, X))
    f2[np.arange(Q)[:, None], idx4[np.arange(Q) % 128 // 16]] = pick8(mo, idx3, 16)
    cc = c0 - f2
    y = pick8(cc, idx, 16)
    return y

@@ -1,0 +1,172 @@
+from contextlib import ExitStack
+
+import concourse.mybir as mybir
+from concourse.masks import make_identity
+
+D, K, T, U, X, I, O, Q = 512, 512, 1024, 1024, 1024, 512, 2048, 128
+FLOPS = 2 * Q * (D * K + K * T + K * U + D * X)
+
+F32 = mybir.dt.float32
+BF16 = mybir.dt.bfloat16
+I32 = mybir.dt.int32
+U32 = mybir.dt.uint32
+U16 = mybir.dt.uint16
+U8 = mybir.dt.uint8
+FP8X4 = mybir.dt.float8_e4m3fn_x4
+FP4X4 = mybir.dt.float4_e2m1fn_x4
+COPY = mybir.ActivationFunctionType.Copy
+MAX = mybir.AluOpType.max
+SUBTRACT = mybir.AluOpType.subtract
+
+P = 128
+PACK = 4
+BANK = 512
+C0_PIECE = 256
+HALF_LIST = I // 2
+HALF_COLS = HALF_LIST // 16
+
+
+def tile_attend_endwrite_sidethree_kernel(
+    tc, states, wq_words, wq_scales, cache_words, cache_scales, draft_words, draft_scales,
+    arch_words, arch_scales, offs, offs2, offs3, offs4, out,
+):
+    nc = tc.nc
+    with ExitStack() as ctx:
+        sb = ctx.enter_context(tc.tile_pool(name="sb", bufs=1))
+        ps = ctx.enter_context(tc.psum_pool(name="ps", bufs=1))
+
+        def bank(index, shape, name):
+            return ps.tile(shape, F32, name=name, tag="bank%d" % index)
+
+        def scale_plane(name, width):
+            plane = sb.tile([P, width], U8, name=name, align_bytes=64)
+            nc.vector.memset(plane[:].bitcast(I32), 0)
+            return plane
+
+        def load_scales(queue, plane, scales):
+            for quad in range(4):
+                queue.dma_start(
+                    plane[32 * quad : 32 * quad + 4, :].bitcast(I32),
+                    scales[0, 4 * quad : 4 * quad + 4, :].bitcast(I32),
+                )
+
+        def load_words(name, words, first, width):
+            tile = sb.tile([P, width], U32, name=name, align_bytes=256)
+            rows = words[0].rearrange("p n t -> p (n t)")
+            nc.sync.dma_start(tile[:].bitcast(I32), rows[:, PACK * first : PACK * (first + width)].bitcast(I32))
+            return tile
+
+        def load_list(name, source):
+            tile = sb.tile([P, I // 16], U16, name=name)
+            nc.sync.dma_start(tile[:], source)
+            return tile
+
+        arch_plane = scale_plane("arch_plane", X)
+        wq_plane = scale_plane("wq_plane", K)
+        cache_plane = scale_plane("cache_plane", T)
+        draft_plane = scale_plane("draft_plane", U)
+
+        states_raw = sb.tile([P, PACK, Q], F32, name="states_raw", align_bytes=256)
+        nc.sync.dma_start(states_raw[:], states.rearrange("(p t) q -> p t q", t=PACK))
+        load_scales(nc.scalar, arch_plane, arch_scales)
+        arch_tiles = [load_words("arch%d" % h, arch_words, h * BANK, BANK) for h in range(X // BANK)]
+        idx = load_list("idx", offs)
+        wq_tile = load_words("wq", wq_words, 0, K)
+        load_scales(nc.sync, wq_plane, wq_scales)
+        idx2 = load_list("idx2", offs2)
+        cache_tile = load_words("cache", cache_words, 0, T)
+        draft_tile = sb.tile([P, 2 * U], U8, name="draft", align_bytes=256)
+        nc.sync.dma_start(draft_tile[:].bitcast(I32), draft_words[0].bitcast(I32))
+        load_scales(nc.sync, cache_plane, cache_scales)
+        load_scales(nc.sync, draft_plane, draft_scales)
+        idx3 = load_list("idx3", offs3)
+        idx4 = load_list("idx4", offs4)
+
+        f1 = sb.tile([P, O], F32, name="f1")
+        nc.vector.memset(f1[:], 0.0)
+        f2 = sb.tile([P, X], F32, name="f2")
+        nc.gpsimd.memset(f2[:], 0.0)
+        identity = sb.tile([P, P], F32, name="identity")
+        make_identity(nc, identity[:])
+
+        states_bf = sb.tile([P, Q, PACK], BF16, name="states_bf", align_bytes=64)
+        states_codes = sb.tile([P, Q], U32, name="states_codes", align_bytes=64)
+        states_plane = sb.tile([P, Q], U8, name="states_plane", align_bytes=64)
+        nc.vector.tensor_copy(states_bf[:], states_raw[:].rearrange("p t q -> p q t"))
+        nc.vector.quantize_mx(
+            out=states_codes[:].bitcast(FP8X4), scales=states_plane[:],
+            in_=states_bf[:].rearrange("p q t -> p (q t)"),
+        )
+
+        c0 = sb.tile([P, X], F32, name="c0")
+        for j in range(X // C0_PIECE):
+            cols = slice(j * C0_PIECE, (j + 1) * C0_PIECE)
+            half, start = divmod(j * C0_PIECE, BANK)
+            acc = bank(j, [P, C0_PIECE], "c0_acc%d" % j)
+            nc.tensor.matmul_mx(
+                out=acc[:], lhsT=states_codes[:].bitcast(FP8X4), lhsT_scale=states_plane[:],
+                rhs=arch_tiles[half][:, start : start + C0_PIECE].bitcast(FP8X4),
+                rhs_scale=arch_plane[:, cols], start=True, stop=True,
+            )
+            if j % 2 == 0:
+                nc.scalar.activation(c0[:, cols], acc[:], COPY)
+            else:
+                nc.vector.tensor_copy(c0[:, cols], acc[:])
+
+        qv_acc = bank(4, [P, K], "qv_acc")
+        nc.tensor.matmul_mx(
+            out=qv_acc[:], lhsT=states_codes[:].bitcast(FP8X4), lhsT_scale=states_plane[:],
+            rhs=wq_tile[:].bitcast(FP8X4), rhs_scale=wq_plane[:], start=True, stop=True,
+        )
+
+        for h in range(2):
+            lcols = slice(h * HALF_COLS, (h + 1) * HALF_COLS)
+            picked = sb.tile([P, HALF_LIST], F32, name="c0_picked%d" % h)
+            nc.vector.tensor_copy(picked[:], c0[:].indirect(idx[:, lcols]))
+            nc.scalar.activation(f1[:].indirect(idx2[:, lcols]), picked[:], COPY)
+
+        qv_rows = sb.tile([P, 2, P, 2], BF16, name="qv_rows", align_bytes=64)
+        nc.vector.tensor_copy(qv_rows[:], qv_acc[:].rearrange("q (p u e) -> q u p e", u=2, e=2))
+        qv_pairs = qv_rows[:].rearrange("q u p e -> q (u p e)").bitcast(F32)
+        turned = bank(5, [P, 2, Q], "turned")
+        for u in range(2):
+            nc.tensor.transpose(turned[:, u, :], qv_pairs[:, u * P : (u + 1) * P], identity[:])
+        qv_bf = sb.tile([P, Q * PACK], BF16, name="qv_bf", align_bytes=64)
+        nc.vector.tensor_copy(
+            qv_bf[:].bitcast(F32).rearrange("p (q u) -> p q u", u=2), turned[:].rearrange("p u q -> p q u")
+        )
+        qv_codes = sb.tile([P, Q], U32, name="qv_codes", align_bytes=64)
+        qv_plane = sb.tile([P, Q], U8, name="qv_plane", align_bytes=64)
+        nc.vector.quantize_mx(out=qv_codes[:].bitcast(FP8X4), scales=qv_plane[:], in_=qv_bf[:])
+
+        mo = sb.tile([P, O], F32, name="mo")
+        for j in range(O // BANK):
+            acc = bank((6, 7, 0, 1)[j], [P, BANK], "ab_acc%d" % j)
+            if j < T // BANK:
+                cols = slice(j * BANK, (j + 1) * BANK)
+                keys = cache_tile[:, cols].bitcast(FP8X4)
+                plane = cache_plane[:, cols]
+            else:
+                first = j * BANK - T
+                keys = draft_tile[:, 2 * first : 2 * (first + BANK)].bitcast(FP4X4)
+                plane = draft_plane[:, first : first + BANK]
+            nc.tensor.matmul_mx(
+                out=acc[:], lhsT=qv_codes[:].bitcast(FP8X4), lhsT_scale=qv_plane[:],
+                rhs=keys, rhs_scale=plane, start=True, stop=True,
+            )
+            page = slice(j * BANK, (j + 1) * BANK)
+            nc.vector.tensor_tensor(mo[:, page], acc[:], f1[:, page], MAX)
+
+        mo_picked = sb.tile([P, I], F32, name="mo_picked")
+        nc.vector.tensor_copy(mo_picked[:], mo[:].indirect(idx3[:]))
+        nc.scalar.activation(f2[:].indirect(idx4[:]), mo_picked[:], COPY)
+
+        cc = sb.tile([P, X], F32, name="cc")
+        nc.vector.tensor_tensor(cc[:], c0[:], f2[:], SUBTRACT)
+
+        res0 = sb.tile([P, HALF_LIST], F32, name="res0")
+        nc.vector.tensor_copy(res0[:], cc[:].indirect(idx[:, 0:HALF_COLS]))
+        nc.sync.dma_start(out[:, 0:HALF_LIST], res0[:])
+        res1 = sb.tile([P, HALF_LIST], F32, name="res1")
+        nc.scalar.activation(res1[:], cc[:].indirect(idx[:, HALF_COLS : 2 * HALF_COLS]), COPY)
+        nc.scalar.dma_start(out[:, HALF_LIST:I], res1[:])

@@ -21,7 +21,8 @@ SUBTRACT = mybir.AluOpType.subtract
 P = 128
 PACK = 4
 BANK = 512
-C0_PIECE = 256
+C0_PIECES = (256, 256, 256, 128, 128)
+CAST_SPLIT = 80
 HALF_LIST = I // 2
 HALF_COLS = HALF_LIST // 16
 
@@ -38,9 +39,9 @@ def tile_attend_endwrite_sidethree_kernel(
         def bank(index, shape, name):
             return ps.tile(shape, F32, name=name, tag="bank%d" % index)
 
-        def scale_plane(name, width):
+        def scale_plane(name, width, engine):
             plane = sb.tile([P, width], U8, name=name, align_bytes=64)
-            nc.vector.memset(plane[:].bitcast(I32), 0)
+            engine.memset(plane[:].bitcast(I32), 0)
             return plane
 
         def load_scales(queue, plane, scales):
@@ -61,51 +62,53 @@ def tile_attend_endwrite_sidethree_kernel(
             nc.sync.dma_start(tile[:], source)
             return tile
 
-        arch_plane = scale_plane("arch_plane", X)
-        wq_plane = scale_plane("wq_plane", K)
-        cache_plane = scale_plane("cache_plane", T)
-        draft_plane = scale_plane("draft_plane", U)
+        arch_plane = scale_plane("arch_plane", X, nc.gpsimd)
+        wq_plane = scale_plane("wq_plane", K, nc.vector)
+        cache_plane = scale_plane("cache_plane", T, nc.gpsimd)
+        draft_plane = scale_plane("draft_plane", U, nc.gpsimd)
 
         states_raw = sb.tile([P, PACK, Q], F32, name="states_raw", align_bytes=256)
         nc.sync.dma_start(states_raw[:], states.rearrange("(p t) q -> p t q", t=PACK))
-        load_scales(nc.scalar, arch_plane, arch_scales)
+        load_scales(nc.sync, arch_plane, arch_scales)
         arch_tiles = [load_words("arch%d" % h, arch_words, h * BANK, BANK) for h in range(X // BANK)]
         idx = load_list("idx", offs)
-        wq_tile = load_words("wq", wq_words, 0, K)
         load_scales(nc.sync, wq_plane, wq_scales)
+        wq_tile = load_words("wq", wq_words, 0, K)
         idx2 = load_list("idx2", offs2)
         cache_tile = load_words("cache", cache_words, 0, T)
+        load_scales(nc.sync, cache_plane, cache_scales)
         draft_tile = sb.tile([P, 2 * U], U8, name="draft", align_bytes=256)
         nc.sync.dma_start(draft_tile[:].bitcast(I32), draft_words[0].bitcast(I32))
-        load_scales(nc.sync, cache_plane, cache_scales)
         load_scales(nc.sync, draft_plane, draft_scales)
         idx3 = load_list("idx3", offs3)
         idx4 = load_list("idx4", offs4)
 
         f1 = sb.tile([P, O], F32, name="f1")
-        nc.vector.memset(f1[:], 0.0)
-        f2 = sb.tile([P, X], F32, name="f2")
-        nc.gpsimd.memset(f2[:], 0.0)
-        identity = sb.tile([P, P], F32, name="identity")
-        make_identity(nc, identity[:])
+        nc.vector.memset(f1[:].bitcast(I32), 0)
 
-        states_bf = sb.tile([P, Q, PACK], BF16, name="states_bf", align_bytes=64)
+        states_bf = sb.tile([P, Q, PACK], BF16, name="states_bf", tag="states_bf_then_identity", align_bytes=64)
         states_codes = sb.tile([P, Q], U32, name="states_codes", align_bytes=64)
         states_plane = sb.tile([P, Q], U8, name="states_plane", align_bytes=64)
-        nc.vector.tensor_copy(states_bf[:], states_raw[:].rearrange("p t q -> p q t"))
+        by_row = states_raw[:].rearrange("p t q -> p q t")
+        nc.vector.tensor_copy(states_bf[:, 0:CAST_SPLIT, :], by_row[:, 0:CAST_SPLIT, :])
+        nc.scalar.activation(states_bf[:, CAST_SPLIT:Q, :], by_row[:, CAST_SPLIT:Q, :], COPY)
         nc.vector.quantize_mx(
             out=states_codes[:].bitcast(FP8X4), scales=states_plane[:],
             in_=states_bf[:].rearrange("p q t -> p (q t)"),
         )
 
+        identity = sb.tile([P, P], F32, name="identity", tag="states_bf_then_identity", align_bytes=64)
+        make_identity(nc, identity[:])
+
         c0 = sb.tile([P, X], F32, name="c0")
-        for j in range(X // C0_PIECE):
-            cols = slice(j * C0_PIECE, (j + 1) * C0_PIECE)
-            half, start = divmod(j * C0_PIECE, BANK)
-            acc = bank(j, [P, C0_PIECE], "c0_acc%d" % j)
+        for j, width in enumerate(C0_PIECES):
+            first = sum(C0_PIECES[:j])
+            cols = slice(first, first + width)
+            half, start = divmod(first, BANK)
+            acc = bank(j, [P, width], "c0_acc%d" % j)
             nc.tensor.matmul_mx(
                 out=acc[:], lhsT=states_codes[:].bitcast(FP8X4), lhsT_scale=states_plane[:],
-                rhs=arch_tiles[half][:, start : start + C0_PIECE].bitcast(FP8X4),
+                rhs=arch_tiles[half][:, start : start + width].bitcast(FP8X4),
                 rhs_scale=arch_plane[:, cols], start=True, stop=True,
             )
             if j % 2 == 0:
@@ -113,25 +116,24 @@ def tile_attend_endwrite_sidethree_kernel(
             else:
                 nc.vector.tensor_copy(c0[:, cols], acc[:])
 
-        qv_acc = bank(4, [P, K], "qv_acc")
+        qv_acc = bank(5, [P, K], "qv_acc")
         nc.tensor.matmul_mx(
             out=qv_acc[:], lhsT=states_codes[:].bitcast(FP8X4), lhsT_scale=states_plane[:],
             rhs=wq_tile[:].bitcast(FP8X4), rhs_scale=wq_plane[:], start=True, stop=True,
         )
 
-        for h in range(2):
-            lcols = slice(h * HALF_COLS, (h + 1) * HALF_COLS)
-            picked = sb.tile([P, HALF_LIST], F32, name="c0_picked%d" % h)
-            nc.vector.tensor_copy(picked[:], c0[:].indirect(idx[:, lcols]))
-            nc.scalar.activation(f1[:].indirect(idx2[:, lcols]), picked[:], COPY)
+        c0_picked = sb.tile([P, I], F32, name="c0_picked")
+        nc.vector.tensor_copy(c0_picked[:, 0:HALF_LIST], c0[:].indirect(idx[:, 0:HALF_COLS]))
+        nc.scalar.activation(c0_picked[:, HALF_LIST:I], c0[:].indirect(idx[:, HALF_COLS : 2 * HALF_COLS]), COPY)
+        nc.scalar.activation(f1[:].indirect(idx2[:]), c0_picked[:], COPY)
 
         qv_rows = sb.tile([P, 2, P, 2], BF16, name="qv_rows", align_bytes=64)
         nc.vector.tensor_copy(qv_rows[:], qv_acc[:].rearrange("q (p u e) -> q u p e", u=2, e=2))
         qv_pairs = qv_rows[:].rearrange("q u p e -> q (u p e)").bitcast(F32)
-        turned = bank(5, [P, 2, Q], "turned")
+        turned = bank(6, [P, 2, Q], "turned")
         for u in range(2):
             nc.tensor.transpose(turned[:, u, :], qv_pairs[:, u * P : (u + 1) * P], identity[:])
-        qv_bf = sb.tile([P, Q * PACK], BF16, name="qv_bf", align_bytes=64)
+        qv_bf = sb.tile([P, Q * PACK], BF16, name="qv_bf", tag="qv_bf_then_f2", align_bytes=64)
         nc.vector.tensor_copy(
             qv_bf[:].bitcast(F32).rearrange("p (q u) -> p q u", u=2), turned[:].rearrange("p u q -> p q u")
         )
@@ -139,9 +141,12 @@ def tile_attend_endwrite_sidethree_kernel(
         qv_plane = sb.tile([P, Q], U8, name="qv_plane", align_bytes=64)
         nc.vector.quantize_mx(out=qv_codes[:].bitcast(FP8X4), scales=qv_plane[:], in_=qv_bf[:])
 
+        f2 = sb.tile([P, X], F32, name="f2", tag="qv_bf_then_f2", align_bytes=64)
+        nc.gpsimd.memset(f2[:], 0.0)
+
         mo = sb.tile([P, O], F32, name="mo")
         for j in range(O // BANK):
-            acc = bank((6, 7, 0, 1)[j], [P, BANK], "ab_acc%d" % j)
+            acc = bank((7, 0, 1, 2)[j], [P, BANK], "ab_acc%d" % j)
             if j < T // BANK:
                 cols = slice(j * BANK, (j + 1) * BANK)
                 keys = cache_tile[:, cols].bitcast(FP8X4)

@@ -39,14 +39,9 @@ def tile_attend_endwrite_sidethree_kernel(
         def bank(index, shape, name):
             return ps.tile(shape, F32, name=name, tag="bank%d" % index)
 
-        def scale_plane(name, width, engine):
-            plane = sb.tile([P, width], U8, name=name, align_bytes=64)
-            engine.memset(plane[:].bitcast(I32), 0)
-            return plane
-
-        def load_scales(queue, plane, scales):
+        def load_scales(plane, scales):
             for quad in range(4):
-                queue.dma_start(
+                nc.sync.dma_start(
                     plane[32 * quad : 32 * quad + 4, :].bitcast(I32),
                     scales[0, 4 * quad : 4 * quad + 4, :].bitcast(I32),
                 )
@@ -62,31 +57,27 @@ def tile_attend_endwrite_sidethree_kernel(
             nc.sync.dma_start(tile[:], source)
             return tile
 
-        arch_plane = scale_plane("arch_plane", X, nc.gpsimd)
-        wq_plane = scale_plane("wq_plane", K, nc.vector)
-        cache_plane = scale_plane("cache_plane", T, nc.gpsimd)
-        draft_plane = scale_plane("draft_plane", U, nc.gpsimd)
+        arch_plane = sb.tile([P, X], U8, name="arch_plane", align_bytes=64)
+        nc.vector.memset(arch_plane[:].bitcast(I32), 0)
+        wq_plane = sb.tile([P, K], U8, name="wq_plane", align_bytes=64)
+        nc.vector.memset(wq_plane[:].bitcast(I32), 0)
+        f1 = sb.tile([P, O], F32, name="f1")
+        nc.vector.memset(f1[:].bitcast(I32), 0)
+        identity = sb.tile([P, P], F32, name="identity")
+        nc.vector.memset(identity[:], 0.0)
+        make_identity(nc, identity[:], nomemset=True)
 
         states_raw = sb.tile([P, PACK, Q], F32, name="states_raw", align_bytes=256)
         nc.sync.dma_start(states_raw[:], states.rearrange("(p t) q -> p t q", t=PACK))
-        load_scales(nc.sync, arch_plane, arch_scales)
-        arch_tiles = [load_words("arch%d" % h, arch_words, h * BANK, BANK) for h in range(X // BANK)]
+        arch_tiles = [load_words("arch0", arch_words, 0, BANK)]
+        load_scales(arch_plane, arch_scales)
+        arch_tiles.append(load_words("arch1", arch_words, BANK, BANK))
         idx = load_list("idx", offs)
-        load_scales(nc.sync, wq_plane, wq_scales)
+        load_scales(wq_plane, wq_scales)
         wq_tile = load_words("wq", wq_words, 0, K)
         idx2 = load_list("idx2", offs2)
-        cache_tile = load_words("cache", cache_words, 0, T)
-        load_scales(nc.sync, cache_plane, cache_scales)
-        draft_tile = sb.tile([P, 2 * U], U8, name="draft", align_bytes=256)
-        nc.sync.dma_start(draft_tile[:].bitcast(I32), draft_words[0].bitcast(I32))
-        load_scales(nc.sync, draft_plane, draft_scales)
-        idx3 = load_list("idx3", offs3)
-        idx4 = load_list("idx4", offs4)
 
-        f1 = sb.tile([P, O], F32, name="f1")
-        nc.vector.memset(f1[:].bitcast(I32), 0)
-
-        states_bf = sb.tile([P, Q, PACK], BF16, name="states_bf", tag="states_bf_then_identity", align_bytes=64)
+        states_bf = sb.tile([P, Q, PACK], BF16, name="states_bf", tag="states_bf_then_page_plane", align_bytes=64)
         states_codes = sb.tile([P, Q], U32, name="states_codes", align_bytes=64)
         states_plane = sb.tile([P, Q], U8, name="states_plane", align_bytes=64)
         by_row = states_raw[:].rearrange("p t q -> p q t")
@@ -97,8 +88,15 @@ def tile_attend_endwrite_sidethree_kernel(
             in_=states_bf[:].rearrange("p q t -> p (q t)"),
         )
 
-        identity = sb.tile([P, P], F32, name="identity", tag="states_bf_then_identity", align_bytes=64)
-        make_identity(nc, identity[:])
+        page_plane = sb.tile([P, O], U8, name="page_plane", tag="states_bf_then_page_plane", align_bytes=64)
+        nc.gpsimd.memset(page_plane[:].bitcast(I32), 0)
+        load_scales(page_plane[:, 0:T], cache_scales)
+        cache_tile = load_words("cache", cache_words, 0, T)
+        draft_tile = sb.tile([P, 2 * U], U8, name="draft", align_bytes=256)
+        nc.sync.dma_start(draft_tile[:].bitcast(I32), draft_words[0].bitcast(I32))
+        load_scales(page_plane[:, T:O], draft_scales)
+        idx3 = load_list("idx3", offs3)
+        idx4 = load_list("idx4", offs4)
 
         c0 = sb.tile([P, X], F32, name="c0")
         for j, width in enumerate(C0_PIECES):
@@ -147,19 +145,16 @@ def tile_attend_endwrite_sidethree_kernel(
         mo = sb.tile([P, O], F32, name="mo")
         for j in range(O // BANK):
             acc = bank((7, 0, 1, 2)[j], [P, BANK], "ab_acc%d" % j)
+            page = slice(j * BANK, (j + 1) * BANK)
             if j < T // BANK:
-                cols = slice(j * BANK, (j + 1) * BANK)
-                keys = cache_tile[:, cols].bitcast(FP8X4)
-                plane = cache_plane[:, cols]
+                keys = cache_tile[:, page].bitcast(FP8X4)
             else:
                 first = j * BANK - T
                 keys = draft_tile[:, 2 * first : 2 * (first + BANK)].bitcast(FP4X4)
-                plane = draft_plane[:, first : first + BANK]
             nc.tensor.matmul_mx(
                 out=acc[:], lhsT=qv_codes[:].bitcast(FP8X4), lhsT_scale=qv_plane[:],
-                rhs=keys, rhs_scale=plane, start=True, stop=True,
+                rhs=keys, rhs_scale=page_plane[:, page], start=True, stop=True,
             )
-            page = slice(j * BANK, (j + 1) * BANK)
             nc.vector.tensor_tensor(mo[:, page], acc[:], f1[:, page], MAX)
 
         mo_picked = sb.tile([P, I], F32, name="mo_picked")

@@ -23,6 +23,7 @@ PACK = 4
 BANK = 512
 C0_PIECES = (256, 256, 256, 128, 128)
 CAST_SPLIT = 80
+CC_SPLIT = 704
 HALF_LIST = I // 2
 HALF_COLS = HALF_LIST // 16
 
@@ -61,6 +62,8 @@ def tile_attend_endwrite_sidethree_kernel(
         nc.vector.memset(arch_plane[:].bitcast(I32), 0)
         wq_plane = sb.tile([P, K], U8, name="wq_plane", align_bytes=64)
         nc.vector.memset(wq_plane[:].bitcast(I32), 0)
+        page_plane = sb.tile([P, O], U8, name="page_plane", align_bytes=64)
+        nc.gpsimd.memset(page_plane[:].bitcast(I32), 0)
         f1 = sb.tile([P, O], F32, name="f1")
         nc.vector.memset(f1[:].bitcast(I32), 0)
         identity = sb.tile([P, P], F32, name="identity")
@@ -73,11 +76,11 @@ def tile_attend_endwrite_sidethree_kernel(
         load_scales(arch_plane, arch_scales)
         arch_tiles.append(load_words("arch1", arch_words, BANK, BANK))
         idx = load_list("idx", offs)
-        load_scales(wq_plane, wq_scales)
         wq_tile = load_words("wq", wq_words, 0, K)
+        load_scales(wq_plane, wq_scales)
         idx2 = load_list("idx2", offs2)
 
-        states_bf = sb.tile([P, Q, PACK], BF16, name="states_bf", tag="states_bf_then_page_plane", align_bytes=64)
+        states_bf = sb.tile([P, Q, PACK], BF16, name="states_bf", align_bytes=64)
         states_codes = sb.tile([P, Q], U32, name="states_codes", align_bytes=64)
         states_plane = sb.tile([P, Q], U8, name="states_plane", align_bytes=64)
         by_row = states_raw[:].rearrange("p t q -> p q t")
@@ -88,10 +91,8 @@ def tile_attend_endwrite_sidethree_kernel(
             in_=states_bf[:].rearrange("p q t -> p (q t)"),
         )
 
-        page_plane = sb.tile([P, O], U8, name="page_plane", tag="states_bf_then_page_plane", align_bytes=64)
-        nc.gpsimd.memset(page_plane[:].bitcast(I32), 0)
-        load_scales(page_plane[:, 0:T], cache_scales)
         cache_tile = load_words("cache", cache_words, 0, T)
+        load_scales(page_plane[:, 0:T], cache_scales)
         draft_tile = sb.tile([P, 2 * U], U8, name="draft", align_bytes=256)
         nc.sync.dma_start(draft_tile[:].bitcast(I32), draft_words[0].bitcast(I32))
         load_scales(page_plane[:, T:O], draft_scales)
@@ -99,6 +100,7 @@ def tile_attend_endwrite_sidethree_kernel(
         idx4 = load_list("idx4", offs4)
 
         c0 = sb.tile([P, X], F32, name="c0")
+        c0_banks = []
         for j, width in enumerate(C0_PIECES):
             first = sum(C0_PIECES[:j])
             cols = slice(first, first + width)
@@ -109,6 +111,7 @@ def tile_attend_endwrite_sidethree_kernel(
                 rhs=arch_tiles[half][:, start : start + width].bitcast(FP8X4),
                 rhs_scale=arch_plane[:, cols], start=True, stop=True,
             )
+            c0_banks.append((first, width, acc))
             if j % 2 == 0:
                 nc.scalar.activation(c0[:, cols], acc[:], COPY)
             else:
@@ -144,7 +147,7 @@ def tile_attend_endwrite_sidethree_kernel(
 
         mo = sb.tile([P, O], F32, name="mo")
         for j in range(O // BANK):
-            acc = bank((7, 0, 1, 2)[j], [P, BANK], "ab_acc%d" % j)
+            acc = bank((7, 3, 4, 5)[j], [P, BANK], "ab_acc%d" % j)
             page = slice(j * BANK, (j + 1) * BANK)
             if j < T // BANK:
                 keys = cache_tile[:, page].bitcast(FP8X4)
@@ -162,7 +165,10 @@ def tile_attend_endwrite_sidethree_kernel(
         nc.scalar.activation(f2[:].indirect(idx4[:]), mo_picked[:], COPY)
 
         cc = sb.tile([P, X], F32, name="cc")
-        nc.vector.tensor_tensor(cc[:], c0[:], f2[:], SUBTRACT)
+        nc.gpsimd.tensor_tensor(cc[:, CC_SPLIT:X], c0[:, CC_SPLIT:X], f2[:, CC_SPLIT:X], SUBTRACT)
+        for first, width, acc in c0_banks[:3]:
+            last = min(first + width, CC_SPLIT)
+            nc.vector.tensor_tensor(cc[:, first:last], acc[:, 0 : last - first], f2[:, first:last], SUBTRACT)
 
         res0 = sb.tile([P, HALF_LIST], F32, name="res0")
         nc.vector.tensor_copy(res0[:], cc[:].indirect(idx[:, 0:HALF_COLS]))

from contextlib import ExitStack

import concourse.mybir as mybir
from concourse.masks import make_identity

D, K, T, U, X, I, O, Q = 512, 512, 1024, 1024, 1024, 512, 2048, 128
FLOPS = 2 * Q * (D * K + K * T + K * U + D * X)

F32 = mybir.dt.float32
BF16 = mybir.dt.bfloat16
I32 = mybir.dt.int32
U32 = mybir.dt.uint32
U16 = mybir.dt.uint16
U8 = mybir.dt.uint8
FP8X4 = mybir.dt.float8_e4m3fn_x4
FP4X4 = mybir.dt.float4_e2m1fn_x4
COPY = mybir.ActivationFunctionType.Copy
MAX = mybir.AluOpType.max
SUBTRACT = mybir.AluOpType.subtract

P = 128
PACK = 4
BANK = 512
C0_PIECES = (256, 256, 256, 128, 128)
CAST_SPLIT = 80
CC_SPLIT = 704
HALF_LIST = I // 2
HALF_COLS = HALF_LIST // 16


def tile_attend_endwrite_sidethree_kernel(
    tc, states, wq_words, wq_scales, cache_words, cache_scales, draft_words, draft_scales,
    arch_words, arch_scales, offs, offs2, offs3, offs4, out,
):
    nc = tc.nc
    with ExitStack() as ctx:
        sb = ctx.enter_context(tc.tile_pool(name="sb", bufs=1))
        ps = ctx.enter_context(tc.psum_pool(name="ps", bufs=1))

        def bank(index, shape, name):
            return ps.tile(shape, F32, name=name, tag="bank%d" % index)

        def load_scales(plane, scales):
            for quad in range(4):
                nc.sync.dma_start(
                    plane[32 * quad : 32 * quad + 4, :].bitcast(I32),
                    scales[0, 4 * quad : 4 * quad + 4, :].bitcast(I32),
                )

        def load_words(name, words, first, width):
            tile = sb.tile([P, width], U32, name=name, align_bytes=256)
            rows = words[0].rearrange("p n t -> p (n t)")
            nc.sync.dma_start(tile[:].bitcast(I32), rows[:, PACK * first : PACK * (first + width)].bitcast(I32))
            return tile

        def load_list(name, source):
            tile = sb.tile([P, I // 16], U16, name=name)
            nc.sync.dma_start(tile[:], source)
            return tile

        arch_plane = sb.tile([P, X], U8, name="arch_plane", align_bytes=64)
        nc.vector.memset(arch_plane[:].bitcast(I32), 0)
        wq_plane = sb.tile([P, K], U8, name="wq_plane", align_bytes=64)
        nc.vector.memset(wq_plane[:].bitcast(I32), 0)
        page_plane = sb.tile([P, O], U8, name="page_plane", align_bytes=64)
        nc.gpsimd.memset(page_plane[:].bitcast(I32), 0)
        f1 = sb.tile([P, O], F32, name="f1")
        nc.vector.memset(f1[:].bitcast(I32), 0)
        identity = sb.tile([P, P], F32, name="identity")
        nc.vector.memset(identity[:], 0.0)
        make_identity(nc, identity[:], nomemset=True)

        states_raw = sb.tile([P, PACK, Q], F32, name="states_raw", align_bytes=256)
        nc.sync.dma_start(states_raw[:], states.rearrange("(p t) q -> p t q", t=PACK))
        arch_tiles = [load_words("arch0", arch_words, 0, BANK)]
        load_scales(arch_plane, arch_scales)
        arch_tiles.append(load_words("arch1", arch_words, BANK, BANK))
        idx = load_list("idx", offs)
        wq_tile = load_words("wq", wq_words, 0, K)
        load_scales(wq_plane, wq_scales)
        idx2 = load_list("idx2", offs2)

        states_bf = sb.tile([P, Q, PACK], BF16, name="states_bf", align_bytes=64)
        states_codes = sb.tile([P, Q], U32, name="states_codes", align_bytes=64)
        states_plane = sb.tile([P, Q], U8, name="states_plane", align_bytes=64)
        by_row = states_raw[:].rearrange("p t q -> p q t")
        nc.vector.tensor_copy(states_bf[:, 0:CAST_SPLIT, :], by_row[:, 0:CAST_SPLIT, :])
        nc.scalar.activation(states_bf[:, CAST_SPLIT:Q, :], by_row[:, CAST_SPLIT:Q, :], COPY)
        nc.vector.quantize_mx(
            out=states_codes[:].bitcast(FP8X4), scales=states_plane[:],
            in_=states_bf[:].rearrange("p q t -> p (q t)"),
        )

        cache_tile = load_words("cache", cache_words, 0, T)
        load_scales(page_plane[:, 0:T], cache_scales)
        draft_tile = sb.tile([P, 2 * U], U8, name="draft", align_bytes=256)
        nc.sync.dma_start(draft_tile[:].bitcast(I32), draft_words[0].bitcast(I32))
        load_scales(page_plane[:, T:O], draft_scales)
        idx3 = load_list("idx3", offs3)
        idx4 = load_list("idx4", offs4)

        c0 = sb.tile([P, X], F32, name="c0")
        c0_banks = []
        for j, width in enumerate(C0_PIECES):
            first = sum(C0_PIECES[:j])
            cols = slice(first, first + width)
            half, start = divmod(first, BANK)
            acc = bank(j, [P, width], "c0_acc%d" % j)
            nc.tensor.matmul_mx(
                out=acc[:], lhsT=states_codes[:].bitcast(FP8X4), lhsT_scale=states_plane[:],
                rhs=arch_tiles[half][:, start : start + width].bitcast(FP8X4),
                rhs_scale=arch_plane[:, cols], start=True, stop=True,
            )
            c0_banks.append((first, width, acc))
            if j % 2 == 0:
                nc.scalar.activation(c0[:, cols], acc[:], COPY)
            else:
                nc.vector.tensor_copy(c0[:, cols], acc[:])

        qv_acc = bank(5, [P, K], "qv_acc")
        nc.tensor.matmul_mx(
            out=qv_acc[:], lhsT=states_codes[:].bitcast(FP8X4), lhsT_scale=states_plane[:],
            rhs=wq_tile[:].bitcast(FP8X4), rhs_scale=wq_plane[:], start=True, stop=True,
        )

        c0_picked = sb.tile([P, I], F32, name="c0_picked")
        nc.vector.tensor_copy(c0_picked[:, 0:HALF_LIST], c0[:].indirect(idx[:, 0:HALF_COLS]))
        nc.scalar.activation(c0_picked[:, HALF_LIST:I], c0[:].indirect(idx[:, HALF_COLS : 2 * HALF_COLS]), COPY)
        nc.scalar.activation(f1[:].indirect(idx2[:]), c0_picked[:], COPY)

        qv_rows = sb.tile([P, 2, P, 2], BF16, name="qv_rows", align_bytes=64)
        nc.vector.tensor_copy(qv_rows[:], qv_acc[:].rearrange("q (p u e) -> q u p e", u=2, e=2))
        qv_pairs = qv_rows[:].rearrange("q u p e -> q (u p e)").bitcast(F32)
        turned = bank(6, [P, 2, Q], "turned")
        for u in range(2):
            nc.tensor.transpose(turned[:, u, :], qv_pairs[:, u * P : (u + 1) * P], identity[:])
        qv_bf = sb.tile([P, Q * PACK], BF16, name="qv_bf", tag="qv_bf_then_f2", align_bytes=64)
        nc.vector.tensor_copy(
            qv_bf[:].bitcast(F32).rearrange("p (q u) -> p q u", u=2), turned[:].rearrange("p u q -> p q u")
        )
        qv_codes = sb.tile([P, Q], U32, name="qv_codes", align_bytes=64)
        qv_plane = sb.tile([P, Q], U8, name="qv_plane", align_bytes=64)
        nc.vector.quantize_mx(out=qv_codes[:].bitcast(FP8X4), scales=qv_plane[:], in_=qv_bf[:])

        f2 = sb.tile([P, X], F32, name="f2", tag="qv_bf_then_f2", align_bytes=64)
        nc.gpsimd.memset(f2[:], 0.0)

        mo = sb.tile([P, O], F32, name="mo")
        for j in range(O // BANK):
            acc = bank((7, 3, 4, 5)[j], [P, BANK], "ab_acc%d" % j)
            page = slice(j * BANK, (j + 1) * BANK)
            if j < T // BANK:
                keys = cache_tile[:, page].bitcast(FP8X4)
            else:
                first = j * BANK - T
                keys = draft_tile[:, 2 * first : 2 * (first + BANK)].bitcast(FP4X4)
            nc.tensor.matmul_mx(
                out=acc[:], lhsT=qv_codes[:].bitcast(FP8X4), lhsT_scale=qv_plane[:],
                rhs=keys, rhs_scale=page_plane[:, page], start=True, stop=True,
            )
            nc.vector.tensor_tensor(mo[:, page], acc[:], f1[:, page], MAX)

        mo_picked = sb.tile([P, I], F32, name="mo_picked")
        nc.vector.tensor_copy(mo_picked[:], mo[:].indirect(idx3[:]))
        nc.scalar.activation(f2[:].indirect(idx4[:]), mo_picked[:], COPY)

        cc = sb.tile([P, X], F32, name="cc")
        nc.gpsimd.tensor_tensor(cc[:, CC_SPLIT:X], c0[:, CC_SPLIT:X], f2[:, CC_SPLIT:X], SUBTRACT)
        for first, width, acc in c0_banks[:3]:
            last = min(first + width, CC_SPLIT)
            nc.vector.tensor_tensor(cc[:, first:last], acc[:, 0 : last - first], f2[:, first:last], SUBTRACT)

        res0 = sb.tile([P, HALF_LIST], F32, name="res0")
        nc.vector.tensor_copy(res0[:], cc[:].indirect(idx[:, 0:HALF_COLS]))
        nc.sync.dma_start(out[:, 0:HALF_LIST], res0[:])
        res1 = sb.tile([P, HALF_LIST], F32, name="res1")
        nc.scalar.activation(res1[:], cc[:].indirect(idx[:, HALF_COLS : 2 * HALF_COLS]), COPY)
        nc.scalar.dma_start(out[:, HALF_LIST:I], res1[:])
